import numpy as np, ml_dtypes
CORES = [76,84,92,100,108,116,124]
N = 7
import mx_ref
NC, G = 128, 4
C = np.float32(0.000771)
A = np.float32(0.021)
BF = ml_dtypes.bfloat16
def cut(t, i, w=512):
    return t[:, w * i:w * i + w]
def tile(rs):
    return np.stack(rs, axis=2).reshape(128, -1).astype(BF)
def layer(w, X):
    out = []
    for i in range(G):
        for t in range(len(X)):
            p = mx_ref.matmul(mx_ref.quantize(cut(w, len(X) * i + t)), X[t])
            z = p if t == 0 else z + p
        out.append(z)
    return out
def silu(z):
    z = z.astype(np.float64); e = np.exp(-np.abs(z))
    return (z * np.where(z >= 0, 1, e) / (1 + e)).astype(np.float32)
def gate(U, V):
    return [(silu(u * A) * v) * C for u, v in zip(U, V)]
def setup_inputs(rng):
    def f(*shape):
        return mx_ref.flush((rng.standard_normal(shape, dtype=np.float32) * np.exp2(rng.integers(-2, 3, shape[:-1] + (1,)))).astype(BF))
    return {"x": f(N, 128, 4 * NC), "u": f(N, 128, G * 512), "v": f(N, 128, G * 512), "w2": f(N, 128, N * 512)}
def setup_inputs_blocks(rng):
    d = setup_inputs(rng)
    for k in ("v", "w2"): d[k] = mx_ref.spread(d[k], rng, 2)
    for k in ("x", "u"): d[k] = mx_ref.spread(d[k], rng, 1)
    return d
def setup_inputs_wide(rng):
    d = setup_inputs(rng)
    for k in ("v", "w2"): d[k] = mx_ref.flush((d[k].astype(np.float32) * np.exp2(rng.integers(-5, 6, (N, 1, 1))).astype(np.float32)).astype(BF))
    return d
def setup_inputs_zeros(rng):
    d = setup_inputs(rng); v = d["x"].reshape(N, 128, -1, 4).copy()
    v[np.broadcast_to((rng.random((N, 1, v.shape[2], 1)) < 0.33), v.shape)] = 0
    d["x"] = v.reshape(d["x"].shape)
    return d
def reference(x, u, v, w2, own=None):
    h = np.zeros((N, 128, 4 * NC), BF)
    for j in range(N):
        X = [mx_ref.quantize(x[j])]
        h[j] = tile(gate(layer(u[j], X), layer(v[j], X)))
    use = h if own is None else own["h"]
    H = [mx_ref.quantize(use[j]) for j in range(N)]
    y = np.zeros((N, 128, NC), np.float32)
    for r in range(N):
        for j in range(N):
            p = mx_ref.matmul(mx_ref.quantize(cut(w2[r], j)), H[j])
            y[r] = p if j == 0 else y[r] + p
    return {"h": h, "y": y}

from concourse.bass import DstId, RemoteDMATransfer
from concourse.mybir import dt, AluOpType, ActivationFunctionType

N = 7
G = 4
NC = 128
TW = 4 * NC
BANK = 512
A_SCALE = 0.021
C_SCALE = 0.000771
WA = 4

SCRATCH = {
    "xb": ("sbuf", [128, TW], "bfloat16"),
    "ub": ("sbuf", [128, G * TW], "bfloat16"),
    "vb": ("sbuf", [128, G * TW], "bfloat16"),
    "wb": ("sbuf", [128, N * TW], "bfloat16"),
    "hb": ("sbuf", [128, TW], "bfloat16"),
    "xq": ("sbuf", [128, NC], "float8_e4m3fn_x4"),
    "xs": ("sbuf", [128, NC], "uint8"),
    "uq": ("sbuf", [128, G * NC], "float8_e4m3fn_x4"),
    "us": ("sbuf", [128, G * NC], "uint8"),
    "vq": ("sbuf", [128, G * NC], "float8_e4m3fn_x4"),
    "vs": ("sbuf", [128, G * NC], "uint8"),
    "wq": ("sbuf", [128, N * NC], "float8_e4m3fn_x4"),
    "ws": ("sbuf", [128, N * NC], "uint8"),
    "hq": ("sbuf", [128, N * NC], "float8_e4m3fn_x4"),
    "hs": ("sbuf", [128, N * NC], "uint8"),
    "sil": ("sbuf", [128, G * NC], "float32"),
    "prod": ("sbuf", [128, G * NC], "float32"),
    "yb": ("sbuf", [128, NC], "float32"),
    "pu": ("psum", [128, G * BANK], "float32"),
    "pv": ("psum", [128, G * BANK], "float32"),
}

SEMAPHORES = (
    ["l_x", "l_u0", "l_u1", "l_v0", "l_v1", "l_wa", "l_wb", "q_x", "q_h", "c_3", "m_y", "c_y", "st_h", "st_y", "sent"]
    + ["q_u%d" % b for b in range(G)] + ["q_v%d" % b for b in range(G)]
    + ["m_u%d" % b for b in range(G)] + ["m_v%d" % b for b in range(G)]
    + ["a_s%d" % b for b in range(G)] + ["a_c%d" % b for b in range(G - 1)] + ["p_%d" % b for b in range(G)]
    + ["q_w%d" % j for j in range(N)] + ["arr%d" % j for j in range(N)]
)


def _mask(topo, src, dests):
    m = topo.mask(src, dests[0])
    for d in dests[1:]:
        m &= topo.mask(src, d)
    return m


def _engines(mask):
    return bin(mask).count("1")


def _plan(T, topo):
    cores = list(T.cores)
    everyone = range(topo.CHIPS * topo.CORES_PER_CHIP)
    feeds, jobs, due, when = [], {}, {}, {}
    for r, c in enumerate(cores):
        others = [(r + k) % N for k in range(1, N)]
        near = [q for q in others if topo.may_write(c, cores[q])]
        far = [q for q in others if q not in near]
        spare = [k for k in everyone if topo.chip(k) == topo.chip(c) and k not in cores]
        port = [k for k in spare if all(topo.may_write(k, cores[q]) for q in far)]
        here = [k for k in port if topo.die(k) == topo.die(c)]
        there = [k for k in port if topo.die(k) != topo.die(c)]
        aside = [k for k in spare if k not in port and topo.die(k) != topo.die(c)]
        e = near[0:2]
        rest = [q for q in others if q not in e]
        a, b = rest[0:2], rest[2:4]
        feeds.append([("s", [there[0], there[1]]), ("c", [here[0], here[1], aside[0]])])
        jobs[there[0]] = (r, "s", [a[0], a[1], b[1]])
        jobs[there[1]] = (r, "s", [b[0], e[0], e[1]])
        jobs[here[0]] = (r, "c", a)
        jobs[here[1]] = (r, "c", b)
        jobs[aside[0]] = (r, "c", e)
        for place, q in enumerate([a[0], b[0], a[1], e[0], b[1], e[1]]):
            when[(q, r)] = place
    for k, (r, kind, dests) in jobs.items():
        n = _engines(_mask(topo, k, [cores[q] for q in dests]))
        for q in dests:
            due[(q, r)] = due.get((q, r), 0) + n
    return feeds, jobs, due, when


def _send(g, T, topo, core, kind, r, dests):
    def view():
        if kind == "c":
            return T.hq[:, NC * r:NC * (r + 1)].bitcast(dt.uint8)
        return T.hs[:, NC * r:NC * (r + 1)]
    mask = _mask(topo, core, dests)
    ids = [DstId(rid=topo.addr(d)[0], pnc=topo.addr(d)[1]) for d in dests]
    g.remote_dma_fused(
        [RemoteDMATransfer(dst_ids=ids, dma_engine_mask=mask, remote_sem=T.sem["arr%d" % r],
                           srcs=[view()], dsts=[view() for _ in dests])],
        local_sem=T.sem.sent)
    return _engines(mask)


def _carrier(g, core, T, topo, feeds, job):
    r, kind, dests = job
    src = T.cores[r]
    group = [ks for kd, ks in feeds[r] if core in ks][0]
    g.wait_ge(T.sem["arr%d" % r], _engines(_mask(topo, src, group)))
    n = _send(g, T, topo, core, kind, r, [T.cores[q] for q in dests])
    g.wait_ge(T.sem.sent, n)


def rank_program(g, core, T, topo):
    feeds, jobs, due, when = _plan(T, topo)
    rank = T.rank_of(core)
    if rank is None:
        if core in jobs:
            _carrier(g, core, T, topo, feeds, jobs[core])
        return
    S = T.sem
    sy, sc, ve, te = g.sync, g.scalar, g.vector, g.tensor
    Act = ActivationFunctionType

    def cols(i, w=NC, n=1):
        return slice(w * i, w * (i + n))

    sc.dma_start(T.xb[:], T.x[:]).then_inc(S.l_x, 16)
    sy.dma_start(T.ub[:, cols(0, TW)], T.u[:, cols(0, TW)]).then_inc(S.l_u0, 16)
    sy.dma_start(T.ub[:, cols(1, TW, G - 1)], T.u[:, cols(1, TW, G - 1)]).then_inc(S.l_u1, 16)
    sy.dma_start(T.vb[:, cols(0, TW, 2)], T.v[:, cols(0, TW, 2)]).then_inc(S.l_v0, 16)
    sy.dma_start(T.vb[:, cols(2, TW, 2)], T.v[:, cols(2, TW, 2)]).then_inc(S.l_v1, 16)
    sy.dma_start(T.wb[:, cols(0, TW, WA)], T.w2[:, cols(0, TW, WA)]).then_inc(S.l_wa, 16)

    g.wait_ge(S.q_h, 1)
    left = 0
    for kind, carriers in feeds[rank]:
        left += _send(g, T, topo, core, kind, rank, carriers)
    g.wait_ge(S.sent, left)

    sy.wait_ge(S.sent, left)
    sy.dma_start(T.wb[:, cols(WA, TW, N - WA)], T.w2[:, cols(WA, TW, N - WA)]).then_inc(S.l_wb, 16)
    sy.wait_ge(S.q_h, 1)
    sy.dma_start(T.h[:], T.hb[:]).then_inc(S.st_h, 16)
    sy.wait_ge(S.c_y, 1)
    sy.dma_start(T.y[:], T.yb[:]).then_inc(S.st_y, 16)
    sy.wait_ge(S.st_h, 16)
    sy.wait_ge(S.st_y, 16)

    def pack(q, s, b, i, sem):
        ve.quantize_mx(q[:, cols(i)], s[:, cols(i)], b[:, cols(i, TW)]).then_inc(sem, 1)

    def gate(b):
        ve.wait_ge(S["a_s%d" % b], 1)
        ve.wait_ge(S["m_v%d" % b], 1)
        ve.tensor_tensor(T.prod[:, cols(b)], T.sil[:, cols(b)], T.pv[:, BANK * b:BANK * b + NC],
                         AluOpType.mult).then_inc(S["p_%d" % b], 1)

    ve.wait_ge(S.l_x, 16)
    pack(T.xq, T.xs, T.xb, 0, S.q_x)
    ve.wait_ge(S.l_u0, 16)
    pack(T.uq, T.us, T.ub, 0, S.q_u0)
    ve.wait_ge(S.l_u1, 16)
    for b in range(1, G):
        pack(T.uq, T.us, T.ub, b, S["q_u%d" % b])
    for half, sem in ((0, S.l_v0), (1, S.l_v1)):
        ve.wait_ge(sem, 16)
        for b in (2 * half, 2 * half + 1):
            pack(T.vq, T.vs, T.vb, b, S["q_v%d" % b])
        for b in (2 * half, 2 * half + 1):
            gate(b)
    last = G - 1
    ve.wait_ge(S["p_%d" % last], 1)
    ve.tensor_scalar(T.hb[:, last:TW:G], T.prod[:, cols(last)], C_SCALE, None, AluOpType.mult).then_inc(S.c_3, 1)
    ve.wait_ge(S.c_3, 1)
    for b in range(last):
        ve.wait_ge(S["a_c%d" % b], 1)
    ve.quantize_mx(T.hq[:, cols(rank)], T.hs[:, cols(rank)], T.hb[:]).then_inc(S.q_h, 1)
    ve.wait_ge(S.l_wa, 16)
    for j in range(WA):
        pack(T.wq, T.ws, T.wb, j, S["q_w%d" % j])
    ve.wait_ge(S.l_wb, 16)
    for j in range(WA, N):
        pack(T.wq, T.ws, T.wb, j, S["q_w%d" % j])
    ve.wait_ge(S.m_y, 1)
    ve.tensor_copy(T.yb[:], T.pu[:, 0:NC]).then_inc(S.c_y, 1)

    for b in range(G):
        sc.wait_ge(S["m_u%d" % b], 1)
        sc.activation(T.sil[:, cols(b)], T.pu[:, BANK * b:BANK * b + NC], Act.Silu,
                      scale=A_SCALE).then_inc(S["a_s%d" % b], 1)
    for b in range(last):
        sc.wait_ge(S["p_%d" % b], 1)
        sc.activation(T.hb[:, b:TW:G], T.prod[:, cols(b)], Act.Copy, scale=C_SCALE).then_inc(S["a_c%d" % b], 1)

    te.wait_ge(S.q_x, 1)
    for q, s, ps, name in ((T.uq, T.us, T.pu, "u"), (T.vq, T.vs, T.pv, "v")):
        for b in range(G):
            te.wait_ge(S["q_%s%d" % (name, b)], 1)
            te.matmul_mx(ps[:, BANK * b:BANK * b + NC], q[:, cols(b)], s[:, cols(b)], T.xq[:], T.xs[:],
                         True, True).then_inc(S["m_%s%d" % (name, b)], 1)
    te.wait_ge(S.a_s0, 1)
    order = [rank] + sorted([j for j in range(N) if j != rank], key=lambda j: when[(rank, j)])
    for i, j in enumerate(order):
        te.wait_ge(S["q_w%d" % j], 1)
        if j == rank:
            te.wait_ge(S.q_h, 1)
        else:
            te.wait_ge(S["arr%d" % j], due[(rank, j)])
        mm = te.matmul_mx(T.pu[:, 0:NC], T.wq[:, cols(j)], T.ws[:, cols(j)], T.hq[:, cols(j)], T.hs[:, cols(j)],
                          i == 0, i == N - 1)
        if i == N - 1:
            mm.then_inc(S.m_y, 1)
